import numpy as np, ml_dtypes
CORES = [6,14,22,30,38,134,142,150,158]
N = 9
KT, HT, TK = 4, 1, 128
def setup_inputs(rng):
    w = (rng.standard_normal((128, KT * HT * 128), dtype=np.float32) / 8).astype(ml_dtypes.bfloat16)
    return {"x": rng.standard_normal((N, 128, KT * TK), dtype=np.float32).astype(ml_dtypes.bfloat16), "w": np.broadcast_to(w, (N,) + w.shape).copy()}
def setup_inputs_big(rng):
    d = setup_inputs(rng)
    for k in ("x", "w"): d[k] = (d[k].astype(np.float32) * 1024.0).astype(d[k].dtype)
    return d
def setup_inputs_small(rng):
    d = setup_inputs(rng)
    for k in ("x", "w"): d[k] = (d[k].astype(np.float32) * (1 / 1024.0)).astype(d[k].dtype)
    return d
def setup_inputs_apart(rng):
    d = setup_inputs(rng)
    f = (10.0 ** rng.permutation(np.linspace(-1.5, 1.5, N))).astype(np.float32).reshape(N, 1, 1)
    for k in ("x",): d[k] = (d[k].astype(np.float32) * f).astype(d[k].dtype)
    return d
def reference(x, w):
    X, W = x.astype(np.float64), w.astype(np.float64)
    def hidden(r):
        return np.stack([np.maximum(sum(W[r][:, 128 * (HT * t + u):128 * (HT * t + u) + 128].T @ X[r][:, TK * t:TK * t + TK] for t in range(KT)), 0.0) for u in range(HT)])
    h = [hidden(r) for r in range(N)]
    y = np.stack([sum(h[(r - 1) % N][u].T @ h[r][u] for u in range(HT)) for r in range(N)])
    return {"y": y.astype(ml_dtypes.bfloat16)}

@@ -1,0 +1,69 @@
+from concourse.mybir import AluOpType
+
+TK = 128
+KT = 4
+
+SCRATCH = {
+    "xs": ("sbuf", [128, KT * TK], "bfloat16"),
+    "ws": ("sbuf", [128, KT * TK], "bfloat16"),
+    "zero": ("sbuf", [128, TK], "float32"),
+    "h": ("sbuf", [128, TK], "bfloat16"),
+    "hp": ("sbuf", [128, TK], "bfloat16"),
+    "ys": ("sbuf", [128, TK], "bfloat16"),
+    "ph": ("psum", [128, 512], "float32"),
+    "py": ("psum", [128, 512], "float32"),
+}
+SEMAPHORES = ["ld", "zr", "mm1", "hr", "arr", "sent", "mm2", "yr", "st"]
+
+
+def _engines(mask):
+    return [1 << b for b in range(mask.bit_length()) if (mask >> b) & 1]
+
+
+def _send_mask(topo, src, dst):
+    m = 0
+    for b in _engines(topo.mask(src, dst)):
+        m |= b
+    return m
+
+
+def rank_program(g, core, T, topo):
+    rank = T.rank_of(core)
+    if rank is None:
+        return
+    n = len(T.cores)
+    nxt = T.cores[(rank + 1) % n]
+    prv = T.cores[(rank - 1) % n]
+    assert topo.may_write(core, nxt)
+    out_mask = _send_mask(topo, core, nxt)
+    n_out = len(_engines(out_mask))
+    n_in = len(_engines(_send_mask(topo, prv, core)))
+    S = T.sem
+
+    g.sync.dma_start(T.xs[:], T.x[:]).then_inc(S.ld, 16)
+    g.scalar.dma_start(T.ws[:], T.w[:]).then_inc(S.ld, 16)
+    g.vector.memset(T.zero[:], 0.0).then_inc(S.zr, 1)
+
+    g.tensor.wait_ge(S.ld, 32)
+    for t in range(KT):
+        mm = g.tensor.matmul(T.ph[:, 0:TK], T.ws[:, t * TK:(t + 1) * TK], T.xs[:, t * TK:(t + 1) * TK],
+                             start=(t == 0), stop=(t == KT - 1))
+    mm.then_inc(S.mm1, 1)
+    g.vector.wait_ge(S.zr, 1)
+    g.vector.wait_ge(S.mm1, 1)
+    g.vector.tensor_tensor(T.h[:], T.ph[:, 0:TK], T.zero[:], AluOpType.max).then_inc(S.hr, 1)
+
+    rid, pid = topo.addr(nxt, core)
+    g.wait_ge(S.hr, 1)
+    g.remote_dma(T.hp[:], T.h[:], S.arr, S.sent, pid, rid, out_mask)
+
+    g.tensor.wait_ge(S.hr, 1)
+    g.tensor.wait_ge(S.arr, n_in)
+    g.tensor.matmul(T.py[:, 0:TK], T.hp[:], T.h[:], start=True, stop=True).then_inc(S.mm2, 1)
+    g.vector.wait_ge(S.mm2, 1)
+    g.vector.tensor_copy(T.ys[:], T.py[:, 0:TK]).then_inc(S.yr, 1)
+    g.sync.wait_ge(S.yr, 1)
+    g.sync.dma_start(T.y[:], T.ys[:]).then_inc(S.st, 16)
+
+    g.wait_ge(S.sent, n_out)
+    g.sync.wait_ge(S.st, 16)

@@ -4,27 +4,30 @@ TK = 128
 KT = 4
 
 SCRATCH = {
-    "xs": ("sbuf", [128, KT * TK], "bfloat16"),
+    "x0": ("sbuf", [128, TK], "bfloat16"),
+    "xr": ("sbuf", [128, (KT - 1) * TK], "bfloat16"),
     "ws": ("sbuf", [128, KT * TK], "bfloat16"),
-    "zero": ("sbuf", [128, TK], "float32"),
+    "zf": ("sbuf", [128, TK], "float32"),
+    "zb": ("sbuf", [128, TK], "bfloat16"),
+    "pb": ("sbuf", [128, TK], "bfloat16"),
     "h": ("sbuf", [128, TK], "bfloat16"),
-    "hp": ("sbuf", [128, TK], "bfloat16"),
+    "hn": ("sbuf", [128, TK], "bfloat16"),
+    "x0p": ("sbuf", [128, TK], "bfloat16"),
+    "pin": ("sbuf", [128, TK], "bfloat16"),
+    "nq": ("sbuf", [128, TK], "bfloat16"),
+    "m": ("sbuf", [128, TK], "bfloat16"),
     "ys": ("sbuf", [128, TK], "bfloat16"),
-    "ph": ("psum", [128, 512], "float32"),
+    "pp": ("psum", [128, 512], "float32"),
+    "pf": ("psum", [128, 512], "float32"),
+    "pq": ("psum", [128, 512], "float32"),
     "py": ("psum", [128, 512], "float32"),
 }
-SEMAPHORES = ["ld", "zr", "mm1", "hr", "arr", "sent", "mm2", "yr", "st"]
+SEMAPHORES = ["ld0", "ld", "zr", "mmp", "mmf", "mmq", "mmy", "pr", "hr", "hnr", "nqr", "mr", "yr",
+              "arr0", "arrp", "sent", "st"]
 
 
-def _engines(mask):
-    return [1 << b for b in range(mask.bit_length()) if (mask >> b) & 1]
-
-
-def _send_mask(topo, src, dst):
-    m = 0
-    for b in _engines(topo.mask(src, dst)):
-        m |= b
-    return m
+def _count(mask):
+    return bin(mask).count("1")
 
 
 def rank_program(g, core, T, topo):
@@ -35,35 +38,64 @@ def rank_program(g, core, T, topo):
     nxt = T.cores[(rank + 1) % n]
     prv = T.cores[(rank - 1) % n]
     assert topo.may_write(core, nxt)
-    out_mask = _send_mask(topo, core, nxt)
-    n_out = len(_engines(out_mask))
-    n_in = len(_engines(_send_mask(topo, prv, core)))
+    out_mask = topo.mask(core, nxt)
+    n_out = _count(out_mask)
+    n_in = _count(topo.mask(prv, core))
+    rid, pid = topo.addr(nxt, core)
     S = T.sem
+    c = slice(0, TK)
 
-    g.sync.dma_start(T.xs[:], T.x[:]).then_inc(S.ld, 16)
+    def w_tile(t):
+        return T.ws[:, t * TK:(t + 1) * TK]
+
+    def x_tile(t):
+        return T.x0[:] if t == 0 else T.xr[:, (t - 1) * TK:t * TK]
+
+    g.sync.dma_start(T.x0[:], T.x[:, 0:TK]).then_inc(S.ld0, 16)
     g.scalar.dma_start(T.ws[:], T.w[:]).then_inc(S.ld, 16)
-    g.vector.memset(T.zero[:], 0.0).then_inc(S.zr, 1)
+    g.sync.dma_start(T.xr[:], T.x[:, TK:KT * TK]).then_inc(S.ld, 16)
+
+    g.wait_ge(S.ld0, 16)
+    g.remote_dma(T.x0p[:], T.x0[:], S.arr0, S.sent, pid, rid, out_mask)
+    g.wait_ge(S.pr, 1)
+    g.remote_dma(T.pin[:], T.pb[:], S.arrp, S.sent, pid, rid, out_mask)
 
     g.tensor.wait_ge(S.ld, 32)
+    for t in range(1, KT):
+        mm = g.tensor.matmul(T.pp[:, c], w_tile(t), x_tile(t), start=(t == 1), stop=(t == KT - 1))
+    mm.then_inc(S.mmp, 1)
+    g.tensor.wait_ge(S.ld0, 16)
     for t in range(KT):
-        mm = g.tensor.matmul(T.ph[:, 0:TK], T.ws[:, t * TK:(t + 1) * TK], T.xs[:, t * TK:(t + 1) * TK],
-                             start=(t == 0), stop=(t == KT - 1))
-    mm.then_inc(S.mm1, 1)
-    g.vector.wait_ge(S.zr, 1)
-    g.vector.wait_ge(S.mm1, 1)
-    g.vector.tensor_tensor(T.h[:], T.ph[:, 0:TK], T.zero[:], AluOpType.max).then_inc(S.hr, 1)
-
-    rid, pid = topo.addr(nxt, core)
-    g.wait_ge(S.hr, 1)
-    g.remote_dma(T.hp[:], T.h[:], S.arr, S.sent, pid, rid, out_mask)
-
+        mm = g.tensor.matmul(T.pf[:, c], w_tile(t), x_tile(t), start=(t == 0), stop=(t == KT - 1))
+    mm.then_inc(S.mmf, 1)
+    g.tensor.wait_ge(S.arr0, n_in)
+    g.tensor.matmul(T.pq[:, c], w_tile(0), T.x0p[:], start=True, stop=True).then_inc(S.mmq, 1)
+    g.tensor.wait_ge(S.hnr, 1)
+    g.tensor.wait_ge(S.nqr, 1)
+    g.tensor.matmul(T.py[:, c], T.nq[:], T.hn[:], start=True, stop=False)
     g.tensor.wait_ge(S.hr, 1)
-    g.tensor.wait_ge(S.arr, n_in)
-    g.tensor.matmul(T.py[:, 0:TK], T.hp[:], T.h[:], start=True, stop=True).then_inc(S.mm2, 1)
-    g.vector.wait_ge(S.mm2, 1)
-    g.vector.tensor_copy(T.ys[:], T.py[:, 0:TK]).then_inc(S.yr, 1)
+    g.tensor.wait_ge(S.mr, 1)
+    g.tensor.matmul(T.py[:, c], T.m[:], T.h[:], start=False, stop=True).then_inc(S.mmy, 1)
+
+    g.vector.memset(T.zf[:], 0.0).then_inc(S.zr, 1)
+    g.vector.memset(T.zb[:], 0.0).then_inc(S.zr, 1)
+    g.vector.wait_ge(S.mmp, 1)
+    g.vector.tensor_copy(T.pb[:], T.pp[:, c]).then_inc(S.pr, 1)
+    g.vector.wait_ge(S.zr, 2)
+    g.vector.wait_ge(S.mmf, 1)
+    g.vector.tensor_tensor(T.h[:], T.pf[:, c], T.zf[:], AluOpType.max).then_inc(S.hr, 1)
+    g.vector.wait_ge(S.hr, 1)
+    g.vector.tensor_tensor(T.hn[:], T.zb[:], T.h[:], AluOpType.subtract).then_inc(S.hnr, 1)
+    g.vector.wait_ge(S.mmq, 1)
+    g.vector.tensor_tensor(T.nq[:], T.zf[:], T.pq[:, c], AluOpType.subtract).then_inc(S.nqr, 1)
+    g.vector.wait_ge(S.nqr, 1)
+    g.vector.wait_ge(S.arrp, n_in)
+    g.vector.tensor_tensor(T.m[:], T.pin[:], T.nq[:], AluOpType.max).then_inc(S.mr, 1)
+    g.vector.wait_ge(S.mmy, 1)
+    g.vector.tensor_copy(T.ys[:], T.py[:, c]).then_inc(S.yr, 1)
+
     g.sync.wait_ge(S.yr, 1)
     g.sync.dma_start(T.y[:], T.ys[:]).then_inc(S.st, 16)
 
-    g.wait_ge(S.sent, n_out)
+    g.wait_ge(S.sent, 2 * n_out)
     g.sync.wait_ge(S.st, 16)

@@ -1,29 +1,29 @@
-from concourse.mybir import AluOpType
+from concourse.mybir import AluOpType, ActivationFunctionType
 
 TK = 128
 KT = 4
+E = 32
+HC = TK // 2
 
 SCRATCH = {
-    "x0": ("sbuf", [128, TK], "bfloat16"),
-    "xr": ("sbuf", [128, (KT - 1) * TK], "bfloat16"),
+    "xs": ("sbuf", [128, KT * TK], "bfloat16"),
     "ws": ("sbuf", [128, KT * TK], "bfloat16"),
-    "zf": ("sbuf", [128, TK], "float32"),
-    "zb": ("sbuf", [128, TK], "bfloat16"),
+    "nw0": ("sbuf", [128, TK], "bfloat16"),
+    "x0p": ("sbuf", [128, E], "bfloat16"),
     "pb": ("sbuf", [128, TK], "bfloat16"),
-    "h": ("sbuf", [128, TK], "bfloat16"),
-    "hn": ("sbuf", [128, TK], "bfloat16"),
-    "x0p": ("sbuf", [128, TK], "bfloat16"),
     "pin": ("sbuf", [128, TK], "bfloat16"),
-    "nq": ("sbuf", [128, TK], "bfloat16"),
-    "m": ("sbuf", [128, TK], "bfloat16"),
+    "h": ("sbuf", [128, TK], "bfloat16"),
+    "qb": ("sbuf", [128, TK], "bfloat16"),
     "ys": ("sbuf", [128, TK], "bfloat16"),
-    "pp": ("psum", [128, 512], "float32"),
+    "ppa": ("psum", [128, 512], "float32"),
+    "ppb": ("psum", [128, 512], "float32"),
     "pf": ("psum", [128, 512], "float32"),
     "pq": ("psum", [128, 512], "float32"),
-    "py": ("psum", [128, 512], "float32"),
+    "pya": ("psum", [128, 512], "float32"),
+    "pyb": ("psum", [128, 512], "float32"),
 }
-SEMAPHORES = ["ld0", "ld", "zr", "mmp", "mmf", "mmq", "mmy", "pr", "hr", "hnr", "nqr", "mr", "yr",
-              "arr0", "arrp", "sent", "st"]
+SEMAPHORES = ["ld0", "ldx", "ldw0", "ldw1", "nw", "zr", "mmpa", "mmpb", "pr", "mmf", "hr", "mmq", "qbr", "mr",
+              "mya", "myb", "yr", "arr0", "arrp", "sent", "st"]
 
 
 def _count(mask):
@@ -44,57 +44,84 @@ def rank_program(g, core, T, topo):
     rid, pid = topo.addr(nxt, core)
     S = T.sem
     c = slice(0, TK)
+    ca = slice(0, E)
+    cb = slice(E, TK)
+    nb = slice(0, TK - E)
+    ch = slice(0, HC)
+    half = (slice(0, HC), slice(HC, TK))
+    mid = (KT // 2) * TK
 
     def w_tile(t):
         return T.ws[:, t * TK:(t + 1) * TK]
 
-    def x_tile(t):
-        return T.x0[:] if t == 0 else T.xr[:, (t - 1) * TK:t * TK]
-
-    g.sync.dma_start(T.x0[:], T.x[:, 0:TK]).then_inc(S.ld0, 16)
-    g.scalar.dma_start(T.ws[:], T.w[:]).then_inc(S.ld, 16)
-    g.sync.dma_start(T.xr[:], T.x[:, TK:KT * TK]).then_inc(S.ld, 16)
+    g.sync.dma_start(T.xs[:, ca], T.x[:, ca]).then_inc(S.ld0, 16)
+    g.scalar.dma_start(T.ws[:, 0:mid], T.w[:, 0:mid]).then_inc(S.ldw0, 16)
+    g.sync.dma_start(T.xs[:, E:KT * TK], T.x[:, E:KT * TK]).then_inc(S.ldx, 16)
+    g.scalar.dma_start(T.ws[:, mid:KT * TK], T.w[:, mid:KT * TK]).then_inc(S.ldw1, 16)
 
     g.wait_ge(S.ld0, 16)
-    g.remote_dma(T.x0p[:], T.x0[:], S.arr0, S.sent, pid, rid, out_mask)
-    g.wait_ge(S.pr, 1)
+    g.remote_dma(T.x0p[:], T.xs[:, ca], S.arr0, S.sent, pid, rid, out_mask)
+    g.wait_ge(S.pr, 2)
     g.remote_dma(T.pin[:], T.pb[:], S.arrp, S.sent, pid, rid, out_mask)
 
-    g.tensor.wait_ge(S.ld, 32)
-    for t in range(1, KT):
-        mm = g.tensor.matmul(T.pp[:, c], w_tile(t), x_tile(t), start=(t == 1), stop=(t == KT - 1))
-    mm.then_inc(S.mmp, 1)
+    def a_product(t):
+        return g.tensor.matmul(T.ppa[:, ca], w_tile(t), T.xs[:, t * TK:t * TK + E], start=(t == 1), stop=(t == KT - 1))
+
+    def b_product(t):
+        return g.tensor.matmul(T.ppb[:, nb], w_tile(t), T.xs[:, t * TK + E:(t + 1) * TK],
+                               start=(t == 0), stop=(t == KT - 1))
+
+    g.tensor.wait_ge(S.ldx, 16)
+    g.tensor.wait_ge(S.ldw0, 16)
+    for t in range(KT // 2):
+        b_product(t)
+    for t in range(1, KT // 2):
+        a_product(t)
+    g.tensor.wait_ge(S.ldw1, 16)
+    for t in range(KT // 2, KT):
+        mm = a_product(t)
+    mm.then_inc(S.mmpa, 1)
+    for t in range(KT // 2, KT):
+        mm = b_product(t)
+    mm.then_inc(S.mmpb, 1)
     g.tensor.wait_ge(S.ld0, 16)
     for t in range(KT):
-        mm = g.tensor.matmul(T.pf[:, c], w_tile(t), x_tile(t), start=(t == 0), stop=(t == KT - 1))
+        mm = g.tensor.matmul(T.pf[:, c], w_tile(t), T.xs[:, t * TK:(t + 1) * TK], start=(t == 0), stop=(t == KT - 1))
     mm.then_inc(S.mmf, 1)
+    g.tensor.wait_ge(S.nw, 1)
     g.tensor.wait_ge(S.arr0, n_in)
-    g.tensor.matmul(T.pq[:, c], w_tile(0), T.x0p[:], start=True, stop=True).then_inc(S.mmq, 1)
-    g.tensor.wait_ge(S.hnr, 1)
-    g.tensor.wait_ge(S.nqr, 1)
-    g.tensor.matmul(T.py[:, c], T.nq[:], T.hn[:], start=True, stop=False)
+    g.tensor.matmul(T.pq[:, ca], T.nw0[:], T.x0p[:], start=True, stop=True).then_inc(S.mmq, 1)
+    ybank = (T.pya, T.pyb)
+    ydone = (S.mya, S.myb)
     g.tensor.wait_ge(S.hr, 1)
+    g.tensor.wait_ge(S.zr, 1)
+    g.tensor.wait_ge(S.qbr, 1)
+    for hf in range(2):
+        g.tensor.matmul(ybank[hf][:, ch], T.qb[:], T.h[:, half[hf]], start=True, stop=False)
+    g.tensor.wait_ge(S.arrp, n_in)
     g.tensor.wait_ge(S.mr, 1)
-    g.tensor.matmul(T.py[:, c], T.m[:], T.h[:], start=False, stop=True).then_inc(S.mmy, 1)
+    for hf in range(2):
+        g.tensor.matmul(ybank[hf][:, ch], T.pin[:], T.h[:, half[hf]], start=False, stop=True).then_inc(ydone[hf], 1)
 
-    g.vector.memset(T.zf[:], 0.0).then_inc(S.zr, 1)
-    g.vector.memset(T.zb[:], 0.0).then_inc(S.zr, 1)
-    g.vector.wait_ge(S.mmp, 1)
-    g.vector.tensor_copy(T.pb[:], T.pp[:, c]).then_inc(S.pr, 1)
-    g.vector.wait_ge(S.zr, 2)
-    g.vector.wait_ge(S.mmf, 1)
-    g.vector.tensor_tensor(T.h[:], T.pf[:, c], T.zf[:], AluOpType.max).then_inc(S.hr, 1)
-    g.vector.wait_ge(S.hr, 1)
-    g.vector.tensor_tensor(T.hn[:], T.zb[:], T.h[:], AluOpType.subtract).then_inc(S.hnr, 1)
+    g.scalar.wait_ge(S.ldw0, 16)
+    g.scalar.activation(T.nw0[:], w_tile(0), ActivationFunctionType.Copy, scale=-1.0).then_inc(S.nw, 1)
+    g.scalar.wait_ge(S.mmf, 1)
+    g.scalar.activation(T.h[:], T.pf[:, c], ActivationFunctionType.Relu).then_inc(S.hr, 1)
+
+    g.vector.memset(T.qb[:, cb], 0.0).then_inc(S.zr, 1)
+    g.vector.wait_ge(S.mmpa, 1)
+    g.vector.tensor_copy(T.pb[:, ca], T.ppa[:, ca]).then_inc(S.pr, 1)
+    g.vector.wait_ge(S.mmpb, 1)
+    g.vector.tensor_scalar(T.pb[:, cb], T.ppb[:, nb], 0.0, None, AluOpType.max).then_inc(S.pr, 1)
     g.vector.wait_ge(S.mmq, 1)
-    g.vector.tensor_tensor(T.nq[:], T.zf[:], T.pq[:, c], AluOpType.subtract).then_inc(S.nqr, 1)
-    g.vector.wait_ge(S.nqr, 1)
+    g.vector.tensor_scalar(T.qb[:, ca], T.pq[:, ca], -1.0, None, AluOpType.mult).then_inc(S.qbr, 1)
     g.vector.wait_ge(S.arrp, n_in)
-    g.vector.tensor_tensor(T.m[:], T.pin[:], T.nq[:], AluOpType.max).then_inc(S.mr, 1)
-    g.vector.wait_ge(S.mmy, 1)
-    g.vector.tensor_copy(T.ys[:], T.py[:, c]).then_inc(S.yr, 1)
+    g.vector.tensor_tensor(T.pin[:, ca], T.pin[:, ca], T.pq[:, ca], AluOpType.max).then_inc(S.mr, 1)
+    for hf in range(2):
+        g.vector.wait_ge(ydone[hf], 1)
+        g.vector.tensor_copy(T.ys[:, half[hf]], ybank[hf][:, ch]).then_inc(S.yr, 1)
 
-    g.sync.wait_ge(S.yr, 1)
+    g.sync.wait_ge(S.yr, 2)
     g.sync.dma_start(T.y[:], T.ys[:]).then_inc(S.st, 16)
 
     g.wait_ge(S.sent, 2 * n_out)

@@ -2,28 +2,32 @@ from concourse.mybir import AluOpType, ActivationFunctionType
 
 TK = 128
 KT = 4
-E = 32
+E = 8
+KQ = 32
 HC = TK // 2
 
 SCRATCH = {
     "xs": ("sbuf", [128, KT * TK], "bfloat16"),
     "ws": ("sbuf", [128, KT * TK], "bfloat16"),
-    "nw0": ("sbuf", [128, TK], "bfloat16"),
+    "xe": ("sbuf", [128, E], "bfloat16"),
+    "nxe": ("sbuf", [128, E], "bfloat16"),
     "x0p": ("sbuf", [128, E], "bfloat16"),
+    "fl": ("sbuf", [128, HC], "bfloat16"),
     "pb": ("sbuf", [128, TK], "bfloat16"),
     "pin": ("sbuf", [128, TK], "bfloat16"),
-    "h": ("sbuf", [128, TK], "bfloat16"),
+    "h": ("sbuf", [128, HC], "bfloat16"),
     "qb": ("sbuf", [128, TK], "bfloat16"),
     "ys": ("sbuf", [128, TK], "bfloat16"),
-    "ppa": ("psum", [128, 512], "float32"),
-    "ppb": ("psum", [128, 512], "float32"),
+    "ph1": ("psum", [128, 512], "float32"),
+    "ph2": ("psum", [128, 512], "float32"),
+    "pqs": ("psum", [128, 512], "float32"),
     "pf": ("psum", [128, 512], "float32"),
     "pq": ("psum", [128, 512], "float32"),
     "pya": ("psum", [128, 512], "float32"),
     "pyb": ("psum", [128, 512], "float32"),
 }
-SEMAPHORES = ["ld0", "ldx", "ldw0", "ldw1", "nw", "zr", "mmpa", "mmpb", "pr", "mmf", "hr", "mmq", "qbr", "mr",
-              "mya", "myb", "yr", "arr0", "arrp", "sent", "st"]
+SEMAPHORES = ["ld0", "ldx", "ldw0", "ldw1", "zx", "nx", "zr", "zf", "mqs", "flr", "mm1", "mm2", "pr", "mmf", "hr", "mmq",
+              "qbr", "mya", "myb", "yr", "arr0", "arrp", "sent", "st"]
 
 
 def _count(mask):
@@ -43,10 +47,7 @@ def rank_program(g, core, T, topo):
     n_in = _count(topo.mask(prv, core))
     rid, pid = topo.addr(nxt, core)
     S = T.sem
-    c = slice(0, TK)
     ca = slice(0, E)
-    cb = slice(E, TK)
-    nb = slice(0, TK - E)
     ch = slice(0, HC)
     half = (slice(0, HC), slice(HC, TK))
     mid = (KT // 2) * TK
@@ -54,69 +55,77 @@ def rank_program(g, core, T, topo):
     def w_tile(t):
         return T.ws[:, t * TK:(t + 1) * TK]
 
-    g.sync.dma_start(T.xs[:, ca], T.x[:, ca]).then_inc(S.ld0, 16)
+    w0q = T.ws[0:KQ, 0:TK]
+
+    g.sync.dma_start(T.xe[0:KQ, :], T.x[0:KQ, ca]).then_inc(S.ld0, 16)
     g.scalar.dma_start(T.ws[:, 0:mid], T.w[:, 0:mid]).then_inc(S.ldw0, 16)
-    g.sync.dma_start(T.xs[:, E:KT * TK], T.x[:, E:KT * TK]).then_inc(S.ldx, 16)
+    g.sync.dma_start(T.xs[:], T.x[:]).then_inc(S.ldx, 16)
     g.scalar.dma_start(T.ws[:, mid:KT * TK], T.w[:, mid:KT * TK]).then_inc(S.ldw1, 16)
 
+    g.wait_ge(S.zx, 2)
     g.wait_ge(S.ld0, 16)
-    g.remote_dma(T.x0p[:], T.xs[:, ca], S.arr0, S.sent, pid, rid, out_mask)
+    g.remote_dma(T.x0p[:], T.xe[:], S.arr0, S.sent, pid, rid, out_mask)
     g.wait_ge(S.pr, 2)
     g.remote_dma(T.pin[:], T.pb[:], S.arrp, S.sent, pid, rid, out_mask)
 
-    def a_product(t):
-        return g.tensor.matmul(T.ppa[:, ca], w_tile(t), T.xs[:, t * TK:t * TK + E], start=(t == 1), stop=(t == KT - 1))
+    def first_half(t, start, stop):
+        return g.tensor.matmul(T.ph1[:, ch], w_tile(t), T.xs[:, t * TK:t * TK + HC], start=start, stop=stop)
 
-    def b_product(t):
-        return g.tensor.matmul(T.ppb[:, nb], w_tile(t), T.xs[:, t * TK + E:(t + 1) * TK],
-                               start=(t == 0), stop=(t == KT - 1))
+    def second_half(t, start, stop):
+        return g.tensor.matmul(T.ph2[:, ch], w_tile(t), T.xs[:, t * TK + HC:(t + 1) * TK], start=start, stop=stop)
 
-    g.tensor.wait_ge(S.ldx, 16)
-    g.tensor.wait_ge(S.ldw0, 16)
-    for t in range(KT // 2):
-        b_product(t)
-    for t in range(1, KT // 2):
-        a_product(t)
-    g.tensor.wait_ge(S.ldw1, 16)
-    for t in range(KT // 2, KT):
-        mm = a_product(t)
-    mm.then_inc(S.mmpa, 1)
-    for t in range(KT // 2, KT):
-        mm = b_product(t)
-    mm.then_inc(S.mmpb, 1)
     g.tensor.wait_ge(S.ld0, 16)
+    g.tensor.wait_ge(S.ldw0, 16)
+    g.tensor.matmul(T.pqs[:, ca], w0q, T.xe[0:KQ, :], start=True, stop=True).then_inc(S.mqs, 1)
+    g.tensor.wait_ge(S.nx, 1)
+    g.tensor.wait_ge(S.ldx, 16)
+    first_half(0, True, False)
+    g.tensor.matmul(T.ph1[:, ca], w0q, T.nxe[0:KQ, :], start=False, stop=False)
+    first_half(1, False, False)
+    second_half(0, True, False)
+    second_half(1, False, False)
+    g.tensor.wait_ge(S.ldw1, 16)
+    first_half(2, False, False)
+    first_half(3, False, True).then_inc(S.mm1, 1)
+    second_half(2, False, False)
+    second_half(3, False, True).then_inc(S.mm2, 1)
     for t in range(KT):
-        mm = g.tensor.matmul(T.pf[:, c], w_tile(t), T.xs[:, t * TK:(t + 1) * TK], start=(t == 0), stop=(t == KT - 1))
+        mm = g.tensor.matmul(T.pf[:, ch], w_tile(t), T.xs[:, t * TK:t * TK + HC], start=(t == 0), stop=(t == KT - 1))
     mm.then_inc(S.mmf, 1)
-    g.tensor.wait_ge(S.nw, 1)
     g.tensor.wait_ge(S.arr0, n_in)
-    g.tensor.matmul(T.pq[:, ca], T.nw0[:], T.x0p[:], start=True, stop=True).then_inc(S.mmq, 1)
+    g.tensor.matmul(T.pq[:, ca], w0q, T.x0p[0:KQ, :], start=True, stop=True).then_inc(S.mmq, 1)
     ybank = (T.pya, T.pyb)
     ydone = (S.mya, S.myb)
+    own = (T.h[:], T.pb[:, half[1]])
     g.tensor.wait_ge(S.hr, 1)
+    g.tensor.wait_ge(S.pr, 2)
     g.tensor.wait_ge(S.zr, 1)
     g.tensor.wait_ge(S.qbr, 1)
     for hf in range(2):
-        g.tensor.matmul(ybank[hf][:, ch], T.qb[:], T.h[:, half[hf]], start=True, stop=False)
+        g.tensor.matmul(ybank[hf][:, ch], T.qb[:], own[hf], start=True, stop=False)
     g.tensor.wait_ge(S.arrp, n_in)
-    g.tensor.wait_ge(S.mr, 1)
     for hf in range(2):
-        g.tensor.matmul(ybank[hf][:, ch], T.pin[:], T.h[:, half[hf]], start=False, stop=True).then_inc(ydone[hf], 1)
+        g.tensor.matmul(ybank[hf][:, ch], T.pin[:], own[hf], start=False, stop=True).then_inc(ydone[hf], 1)
 
-    g.scalar.wait_ge(S.ldw0, 16)
-    g.scalar.activation(T.nw0[:], w_tile(0), ActivationFunctionType.Copy, scale=-1.0).then_inc(S.nw, 1)
     g.scalar.wait_ge(S.mmf, 1)
-    g.scalar.activation(T.h[:], T.pf[:, c], ActivationFunctionType.Relu).then_inc(S.hr, 1)
+    g.scalar.activation(T.h[:], T.pf[:, ch], ActivationFunctionType.Relu).then_inc(S.hr, 1)
 
-    g.vector.memset(T.qb[:, cb], 0.0).then_inc(S.zr, 1)
-    g.vector.wait_ge(S.mmpa, 1)
-    g.vector.tensor_copy(T.pb[:, ca], T.ppa[:, ca]).then_inc(S.pr, 1)
-    g.vector.wait_ge(S.mmpb, 1)
-    g.vector.tensor_scalar(T.pb[:, cb], T.ppb[:, nb], 0.0, None, AluOpType.max).then_inc(S.pr, 1)
+    g.vector.memset(T.xe[KQ:2 * KQ, :], 0.0).then_inc(S.zx, 1)
+    g.vector.memset(T.xe[2 * KQ:128, :], 0.0).then_inc(S.zx, 1)
+    g.vector.memset(T.fl[:, E:HC], 0.0).then_inc(S.zf, 1)
+    g.vector.memset(T.qb[:, E:TK], 0.0).then_inc(S.zr, 1)
+    g.vector.wait_ge(S.ld0, 16)
+    g.vector.tensor_scalar(T.nxe[0:KQ, :], T.xe[0:KQ, :], -1.0, None, AluOpType.mult).then_inc(S.nx, 1)
+    g.vector.wait_ge(S.mqs, 1)
+    g.vector.tensor_scalar(T.fl[:, ca], T.pqs[:, ca], -1.0, None, AluOpType.mult).then_inc(S.flr, 1)
+    g.vector.wait_ge(S.zf, 1)
+    g.vector.wait_ge(S.flr, 1)
+    g.vector.wait_ge(S.mm1, 1)
+    g.vector.tensor_tensor(T.pb[:, half[0]], T.ph1[:, ch], T.fl[:], AluOpType.max).then_inc(S.pr, 1)
+    g.vector.wait_ge(S.mm2, 1)
+    g.vector.tensor_scalar(T.pb[:, half[1]], T.ph2[:, ch], 0.0, None, AluOpType.max).then_inc(S.pr, 1)
     g.vector.wait_ge(S.mmq, 1)
-    g.vector.tensor_scalar(T.qb[:, ca], T.pq[:, ca], -1.0, None, AluOpType.mult).then_inc(S.qbr, 1)
-    g.vector.wait_ge(S.arrp, n_in)
-    g.vector.tensor_tensor(T.pin[:, ca], T.pin[:, ca], T.pq[:, ca], AluOpType.max).then_inc(S.mr, 1)
+    g.vector.tensor_copy(T.qb[:, ca], T.pq[:, ca]).then_inc(S.qbr, 1)
     for hf in range(2):
         g.vector.wait_ge(ydone[hf], 1)
         g.vector.tensor_copy(T.ys[:, half[hf]], ybank[hf][:, ch]).then_inc(S.yr, 1)

from concourse.mybir import AluOpType, ActivationFunctionType

TK = 128
KT = 4
E = 8
KQ = 32
HC = TK // 2

SCRATCH = {
    "xs": ("sbuf", [128, KT * TK], "bfloat16"),
    "ws": ("sbuf", [128, KT * TK], "bfloat16"),
    "xe": ("sbuf", [128, E], "bfloat16"),
    "nxe": ("sbuf", [128, E], "bfloat16"),
    "x0p": ("sbuf", [128, E], "bfloat16"),
    "fl": ("sbuf", [128, HC], "bfloat16"),
    "pb": ("sbuf", [128, TK], "bfloat16"),
    "pin": ("sbuf", [128, TK], "bfloat16"),
    "h": ("sbuf", [128, HC], "bfloat16"),
    "qb": ("sbuf", [128, TK], "bfloat16"),
    "ys": ("sbuf", [128, TK], "bfloat16"),
    "ph1": ("psum", [128, 512], "float32"),
    "ph2": ("psum", [128, 512], "float32"),
    "pqs": ("psum", [128, 512], "float32"),
    "pf": ("psum", [128, 512], "float32"),
    "pq": ("psum", [128, 512], "float32"),
    "pya": ("psum", [128, 512], "float32"),
    "pyb": ("psum", [128, 512], "float32"),
}
SEMAPHORES = ["ld0", "ldx", "ldw0", "ldw1", "zx", "nx", "zr", "zf", "mqs", "flr", "mm1", "mm2", "pr", "mmf", "hr", "mmq",
              "qbr", "mya", "myb", "yr", "arr0", "arrp", "sent", "st"]


def _count(mask):
    return bin(mask).count("1")


def rank_program(g, core, T, topo):
    rank = T.rank_of(core)
    if rank is None:
        return
    n = len(T.cores)
    nxt = T.cores[(rank + 1) % n]
    prv = T.cores[(rank - 1) % n]
    assert topo.may_write(core, nxt)
    out_mask = topo.mask(core, nxt)
    n_out = _count(out_mask)
    n_in = _count(topo.mask(prv, core))
    rid, pid = topo.addr(nxt, core)
    S = T.sem
    ca = slice(0, E)
    ch = slice(0, HC)
    half = (slice(0, HC), slice(HC, TK))
    mid = (KT // 2) * TK

    def w_tile(t):
        return T.ws[:, t * TK:(t + 1) * TK]

    w0q = T.ws[0:KQ, 0:TK]

    g.sync.dma_start(T.xe[0:KQ, :], T.x[0:KQ, ca]).then_inc(S.ld0, 16)
    g.scalar.dma_start(T.ws[:, 0:mid], T.w[:, 0:mid]).then_inc(S.ldw0, 16)
    g.sync.dma_start(T.xs[:], T.x[:]).then_inc(S.ldx, 16)
    g.scalar.dma_start(T.ws[:, mid:KT * TK], T.w[:, mid:KT * TK]).then_inc(S.ldw1, 16)

    g.wait_ge(S.zx, 2)
    g.wait_ge(S.ld0, 16)
    g.remote_dma(T.x0p[:], T.xe[:], S.arr0, S.sent, pid, rid, out_mask)
    g.wait_ge(S.pr, 2)
    g.remote_dma(T.pin[:], T.pb[:], S.arrp, S.sent, pid, rid, out_mask)

    def first_half(t, start, stop):
        return g.tensor.matmul(T.ph1[:, ch], w_tile(t), T.xs[:, t * TK:t * TK + HC], start=start, stop=stop)

    def second_half(t, start, stop):
        return g.tensor.matmul(T.ph2[:, ch], w_tile(t), T.xs[:, t * TK + HC:(t + 1) * TK], start=start, stop=stop)

    g.tensor.wait_ge(S.ld0, 16)
    g.tensor.wait_ge(S.ldw0, 16)
    g.tensor.matmul(T.pqs[:, ca], w0q, T.xe[0:KQ, :], start=True, stop=True).then_inc(S.mqs, 1)
    g.tensor.wait_ge(S.nx, 1)
    g.tensor.wait_ge(S.ldx, 16)
    first_half(0, True, False)
    g.tensor.matmul(T.ph1[:, ca], w0q, T.nxe[0:KQ, :], start=False, stop=False)
    first_half(1, False, False)
    second_half(0, True, False)
    second_half(1, False, False)
    g.tensor.wait_ge(S.ldw1, 16)
    first_half(2, False, False)
    first_half(3, False, True).then_inc(S.mm1, 1)
    second_half(2, False, False)
    second_half(3, False, True).then_inc(S.mm2, 1)
    for t in range(KT):
        mm = g.tensor.matmul(T.pf[:, ch], w_tile(t), T.xs[:, t * TK:t * TK + HC], start=(t == 0), stop=(t == KT - 1))
    mm.then_inc(S.mmf, 1)
    g.tensor.wait_ge(S.arr0, n_in)
    g.tensor.matmul(T.pq[:, ca], w0q, T.x0p[0:KQ, :], start=True, stop=True).then_inc(S.mmq, 1)
    ybank = (T.pya, T.pyb)
    ydone = (S.mya, S.myb)
    own = (T.h[:], T.pb[:, half[1]])
    g.tensor.wait_ge(S.hr, 1)
    g.tensor.wait_ge(S.pr, 2)
    g.tensor.wait_ge(S.zr, 1)
    g.tensor.wait_ge(S.qbr, 1)
    for hf in range(2):
        g.tensor.matmul(ybank[hf][:, ch], T.qb[:], own[hf], start=True, stop=False)
    g.tensor.wait_ge(S.arrp, n_in)
    for hf in range(2):
        g.tensor.matmul(ybank[hf][:, ch], T.pin[:], own[hf], start=False, stop=True).then_inc(ydone[hf], 1)

    g.scalar.wait_ge(S.mmf, 1)
    g.scalar.activation(T.h[:], T.pf[:, ch], ActivationFunctionType.Relu).then_inc(S.hr, 1)

    g.vector.memset(T.xe[KQ:2 * KQ, :], 0.0).then_inc(S.zx, 1)
    g.vector.memset(T.xe[2 * KQ:128, :], 0.0).then_inc(S.zx, 1)
    g.vector.memset(T.fl[:, E:HC], 0.0).then_inc(S.zf, 1)
    g.vector.memset(T.qb[:, E:TK], 0.0).then_inc(S.zr, 1)
    g.vector.wait_ge(S.ld0, 16)
    g.vector.tensor_scalar(T.nxe[0:KQ, :], T.xe[0:KQ, :], -1.0, None, AluOpType.mult).then_inc(S.nx, 1)
    g.vector.wait_ge(S.mqs, 1)
    g.vector.tensor_scalar(T.fl[:, ca], T.pqs[:, ca], -1.0, None, AluOpType.mult).then_inc(S.flr, 1)
    g.vector.wait_ge(S.zf, 1)
    g.vector.wait_ge(S.flr, 1)
    g.vector.wait_ge(S.mm1, 1)
    g.vector.tensor_tensor(T.pb[:, half[0]], T.ph1[:, ch], T.fl[:], AluOpType.max).then_inc(S.pr, 1)
    g.vector.wait_ge(S.mm2, 1)
    g.vector.tensor_scalar(T.pb[:, half[1]], T.ph2[:, ch], 0.0, None, AluOpType.max).then_inc(S.pr, 1)
    g.vector.wait_ge(S.mmq, 1)
    g.vector.tensor_copy(T.qb[:, ca], T.pq[:, ca]).then_inc(S.qbr, 1)
    for hf in range(2):
        g.vector.wait_ge(ydone[hf], 1)
        g.vector.tensor_copy(T.ys[:, half[hf]], ybank[hf][:, ch]).then_inc(S.yr, 1)

    g.sync.wait_ge(S.yr, 2)
    g.sync.dma_start(T.y[:], T.ys[:]).then_inc(S.st, 16)

    g.wait_ge(S.sent, 2 * n_out)
    g.sync.wait_ge(S.st, 16)
